import numpy as np
import ml_dtypes


def mxq(x, axis, fmt="e4m3"):
    dtype, down = {"e4m3": (ml_dtypes.float8_e4m3fn, 7), "e5m2": (ml_dtypes.float8_e5m2, 14)}[fmt]
    v = np.moveaxis(np.asarray(x, np.float32).astype(ml_dtypes.bfloat16).astype(np.float64), axis, -1)
    blocks = v.reshape(v.shape[:-1] + (-1, 32))
    amax = np.abs(blocks).max(-1, keepdims=True)
    byte = np.maximum(np.where(amax > 0, np.frexp(amax)[1] - 1 + 127, 0) - down, 1)
    scale = np.exp2(byte - 127.0)
    codes = (blocks / scale).astype(np.float32).astype(dtype).astype(np.float64)
    return np.moveaxis((codes * scale).reshape(v.shape), -1, axis)


WIDE = False


def mx_kscale(k):
    if not WIDE:
        return np.ones(k)
    levels = np.array([10, -10, 5, -5, 0])
    if k % 512:
        return np.exp2(np.random.permutation(np.resize(levels, k // 32))).repeat(32)
    a = np.empty((k // 512, 16))
    for p in range(k // 512):
        a[p, :8] = np.random.permutation(np.resize(levels, 8))
        for g in range(8):
            far = levels[np.abs(levels - a[p, g]) >= 10]
            a[p, g + 8] = far[np.random.randint(len(far))]
    return np.exp2(a.ravel()).repeat(32)


def f64(x):
    return np.asarray(x).astype(np.float64)


def striped(idx):
    return np.tile(idx.reshape(-1, 16).T, (8, 1)).astype(np.uint16)


def unstriped(offs):
    return offs[:16].T.reshape(-1).astype(np.int64)


def striped8(idx):
    return np.concatenate([x.reshape(-1, 16).T for x in idx]).astype(np.uint16)


def runs(offs, k):
    lists = np.stack([offs[16 * r : 16 * r + 16].T.reshape(-1) for r in range(8)]).astype(np.int64)
    return lists[np.arange(k) % 512 // 64]


def pack_weight(w):
    k, n = w.shape
    w = f64(np.asarray(w, np.float32).astype(ml_dtypes.bfloat16)).reshape(k // 32, 32, n)
    amax = np.abs(w).max(1)
    byte = np.clip(np.where(amax > 0, np.frexp(amax)[1] - 1 + 127 - 7, 1), 1, 254)
    scaled = (w * np.exp2(127.0 - byte)[:, None, :]).reshape(k, n).astype(np.float32)
    words = np.ascontiguousarray(scaled.reshape(k // 512, 128, 4, n).transpose(0, 1, 3, 2)).astype(ml_dtypes.float8_e4m3fn).view(np.uint8)
    return words, np.ascontiguousarray(byte.astype(np.uint8).reshape(k // 512, 16, n))


def unpack_weight(words, scales):
    g, p, n, _ = words.shape
    vals = np.ascontiguousarray(words).view(ml_dtypes.float8_e4m3fn).astype(np.float64) * np.repeat(np.exp2(scales.astype(np.float64) - 127.0), 8, axis=1)[..., None]
    return vals.transpose(0, 1, 3, 2).reshape(g * 512, n)


E2M1 = np.array([0.0, 0.5, 1.0, 1.5, 2.0, 3.0, 4.0, 6.0, -0.0, -0.5, -1.0, -1.5, -2.0, -3.0, -4.0, -6.0])


def pack_fp4(w):
    k, n = w.shape
    w = f64(np.asarray(w, np.float32).astype(ml_dtypes.bfloat16)).reshape(k // 32, 32, n)
    amax = np.abs(w).max(1)
    mant, ex = np.frexp(amax / 6.0)
    byte = np.clip(np.where(amax > 0, np.where(mant > 0.5, ex, ex - 1) + 127, 1), 1, 254)
    scaled = (w * np.exp2(127.0 - byte)[:, None, :]).reshape(k, n).astype(np.float32)
    c = np.ascontiguousarray(scaled.reshape(k // 512, 128, 4, n).transpose(0, 1, 3, 2)).astype(ml_dtypes.float4_e2m1fn).view(np.uint8) & 0xF
    words = (c[..., 0::2] | (c[..., 1::2] << 4)).reshape(k // 512, 128, 2 * n)
    return np.ascontiguousarray(words), np.ascontiguousarray(byte.astype(np.uint8).reshape(k // 512, 16, n))


def unpack_fp4(words, scales):
    g, _, n = scales.shape
    words = np.ascontiguousarray(words).reshape(g, 128, n, 2)
    nib = np.empty((g, 128, n, 4), np.uint8)
    nib[..., 0::2] = words & 0xF
    nib[..., 1::2] = words >> 4
    vals = E2M1[nib] * np.repeat(np.exp2(scales.astype(np.float64) - 127.0), 8, axis=1)[..., None]
    return vals.transpose(0, 1, 3, 2).reshape(g * 512, n)


def planes(y):
    n, m = y.shape
    v = y.astype(np.float32).astype(ml_dtypes.bfloat16).astype(np.float64).reshape(n // 32, 32, m)
    top = np.abs(v).max(1)
    byte = np.clip(np.where(top > 0, np.frexp(top)[1] - 1 + 127 - 7, 1), 1, 254)
    codes = (v * np.exp2(127.0 - byte)[:, None, :]).reshape(n, m).astype(np.float32).astype(ml_dtypes.float8_e4m3fn).view(np.uint8)
    words = codes.reshape(n // 512, 128, 4, m).transpose(0, 1, 3, 2)
    return np.ascontiguousarray(words), np.ascontiguousarray(byte.astype(np.uint8).reshape(n // 512, 16, m))


K, T, S, V, H = 512, 2048, 512, 512, 512


def setup_inputs():
    n = np.random.standard_normal
    s = mx_kscale(K)[:, None]
    u = mx_kscale(S)
    packed_xT = pack_weight(n((K, T)) * s)
    packed_w1 = pack_fp4(n((K, H)) / np.sqrt(K) / s)
    packed_w2 = pack_fp4(n((K, H)) / np.sqrt(K) / s)
    return {
        "x_words": packed_xT[0],
        "x_scales": packed_xT[1],
        "w1_words": packed_w1[0],
        "w1_scales": packed_w1[1],
        "w2_words": packed_w2[0],
        "w2_scales": packed_w2[1],
        "tau": np.random.uniform(0.3, 0.9, (H, 1)).astype(np.float32),
        "tau2": np.random.uniform(0.3, 0.9, (H, 1)).astype(np.float32),
        "tau3": np.random.uniform(0.3, 0.9, (H, 1)).astype(np.float32),
        "ga": (np.random.uniform(0.5, 1.5, (H, 1)) * u[:, None]).astype(np.float32),
        "gb": (np.random.uniform(0.5, 1.5, (H, 1)) / u[:, None]).astype(np.float32),
        "tau4": np.random.uniform(0.3, 0.9, (S, 1)).astype(np.float32),
        "offs": striped8(np.random.randint(0, T, (8, S))),
        "two": striped(np.random.permutation(T)[:V]),
        "n1": striped8(np.stack([np.random.permutation(S) for _ in range(8)])),
        "n2": striped8(np.stack([np.random.permutation(S) for _ in range(8)])),
        "n3": striped8(np.stack([np.random.permutation(V) for _ in range(8)])),
        "n4": striped8(np.stack([np.random.permutation(V) for _ in range(8)])),
        "n5": striped8(np.stack([np.random.permutation(V) for _ in range(8)])),
    }


def reference(x_words, x_scales, w1_words, w1_scales, w2_words, w2_scales, tau, tau2, tau3, ga, gb, tau4, offs, two, n1, n2, n3, n4, n5):
    xq = unpack_weight(x_words, x_scales)[np.arange(K)[:, None], runs(offs, K)]
    a = unpack_fp4(w1_words, w1_scales).T @ xq
    top = a.max(axis=1, keepdims=True)
    ea = np.exp(f64(tau) * (a[np.arange(H)[:, None], runs(n1, H)] - top))
    low = a.min(axis=1, keepdims=True)
    ea2 = np.exp(f64(tau2) * (low - (a[np.arange(H)[:, None], runs(n2, H)])))
    z = f64(ga) * (1.5 * (a * (ea + ea2)))
    x_two = unpack_weight(x_words, x_scales)[:, unstriped(two)]
    b = unpack_fp4(w2_words, w2_scales).T @ x_two
    top2 = b.max(axis=1, keepdims=True)
    own = np.exp(f64(tau3) * (b - top2))
    ea3 = np.exp(f64(tau3) * (b[np.arange(H)[:, None], runs(n3, H)] - top2))
    z2 = f64(gb) * ((2.0 * (b * own)) / (own + ea3 + 0.25))
    s = 0.0625 * ((mxq(z, 0, "e4m3").T @ mxq(z2, 0, "e4m3")))
    sq = (s) ** 2
    ea4 = np.exp(-1.0 * (f64(tau4) * (sq[np.arange(S)[:, None], runs(n4, S)])))
    out_0 = s * ea4 - (0.5 * (s[np.arange(S)[:, None], runs(n5, S)]))
    return (out_0,) + planes(out_0)

@@ -1,0 +1,296 @@
+from contextlib import ExitStack
+
+import concourse.mybir as mybir
+
+K, T, S, V, H = 512, 2048, 512, 512, 512
+FLOPS = 3 * 2 * 512 * 512 * 512
+
+F32 = mybir.dt.float32
+BF16 = mybir.dt.bfloat16
+I32 = mybir.dt.int32
+U32 = mybir.dt.uint32
+U16 = mybir.dt.uint16
+U8 = mybir.dt.uint8
+FP8X4 = mybir.dt.float8_e4m3fn_x4
+FP4X4 = mybir.dt.float4_e2m1fn_x4
+ALU = mybir.AluOpType
+ACT = mybir.ActivationFunctionType
+AX = mybir.AxisListType
+
+P = 128
+PACK = 4
+N = 512
+WIN = 1024
+
+
+def tile_picked_hkqedfeshega_none_po_kernel(
+    tc, x_words, x_scales, w1_words, w1_scales, w2_words, w2_scales,
+    tau, tau2, tau3, ga, gb, tau4, offs, two, n1, n2, n3, n4, n5,
+    out_0, out_1, out_2,
+):
+    nc = tc.nc
+    with ExitStack() as ctx:
+        held = ctx.enter_context(tc.tile_pool(name="held", bufs=1))
+        ring = ctx.enter_context(tc.tile_pool(name="ring", bufs=2))
+        psum = ctx.enter_context(tc.psum_pool(name="psum", bufs=1))
+
+        def load_list(src, name):
+            lst = held.tile([P, N // 16], U16, name=name)
+            nc.sync.dma_start(lst[:], src)
+            return lst
+
+        def load_rows(src, name):
+            vec = held.tile([P, PACK], F32, name=name)
+            nc.gpsimd.dma_start(vec[:], src.rearrange("(p t) o -> p (t o)", t=PACK))
+            return vec
+
+        def cleared_bytes(width, name):
+            raw = held.tile([P, width], U8, name=name)
+            nc.gpsimd.memset(raw[:].bitcast(I32), 0)
+            return raw
+
+        def load_weight_scales(queues, raw, src):
+            rows = src[0].bitcast(I32)
+            for q in range(4):
+                queues[q].dma_start(raw[32 * q : 32 * q + 4, :].bitcast(I32), rows[4 * q : 4 * q + 4, :])
+
+        def deal_weight(raw_words, raw_scales, name):
+            words = held.tile([P, 2 * H], U8, name=name + "_words", align_bytes=64)
+            scales = held.tile([P, H], U8, name=name + "_scales", align_bytes=64)
+            nc.scalar.copy(
+                words[:].bitcast(U16).rearrange("p (t m) -> p m t", t=PACK),
+                raw_words[:].bitcast(U16).rearrange("p (m t) -> p m t", t=PACK),
+            )
+            nc.vector.tensor_copy(
+                scales[:].rearrange("p (t m) -> p m t", t=PACK),
+                raw_scales[:].rearrange("p (m t) -> p m t", t=PACK),
+            )
+            return words, scales
+
+        xs = cleared_bytes(T, "xs")
+        w2s_raw = cleared_bytes(H, "w2s_raw")
+        w1s_raw = cleared_bytes(H, "w1s_raw")
+        two_l = load_list(two, "two_l")
+        offs_l = load_list(offs, "offs_l")
+        n3_l = load_list(n3, "n3_l")
+        xw = held.tile([P, T], I32, name="xw")
+        nc.sync.dma_start(xw[:], x_words[0].rearrange("p n r -> p (n r)").bitcast(I32))
+        xs_rows = x_scales[0].bitcast(I32)
+        by2 = xs_rows.rearrange("(r j) c -> j r c", j=2)
+        by4 = xs_rows.rearrange("(q j) c -> j q c", j=4)
+        for j in (0, 1):
+            nc.sync.dma_start(xs[j:P:16, :].bitcast(I32), by2[j])
+        for j in (2, 3):
+            nc.sync.dma_start(xs[j:P:32, :].bitcast(I32), by4[j])
+        w2_raw = held.tile([P, 2 * H], U8, name="w2_raw")
+        nc.sync.dma_start(w2_raw[:].bitcast(I32), w2_words[0].bitcast(I32))
+        load_weight_scales((nc.sync, nc.sync, nc.gpsimd, nc.gpsimd), w2s_raw, w2_scales)
+        tau3_t = load_rows(tau3, "tau3_t")
+        w1_raw = held.tile([P, 2 * H], U8, name="w1_raw")
+        nc.sync.dma_start(w1_raw[:].bitcast(I32), w1_words[0].bitcast(I32))
+        load_weight_scales((nc.sync,) * 4, w1s_raw, w1_scales)
+        tau_t = load_rows(tau, "tau_t")
+        tau2_t = load_rows(tau2, "tau2_t")
+        n1_l = load_list(n1, "n1_l")
+        n2_l = load_list(n2, "n2_l")
+        n4_l = load_list(n4, "n4_l")
+        n5_l = load_list(n5, "n5_l")
+        ga_t = load_rows(ga, "ga_t")
+        gb_t = load_rows(gb, "gb_t")
+        tau4_t = load_rows(tau4, "tau4_t")
+
+        def scaled(vec, factor, name):
+            res = held.tile([P, PACK], F32, name=name)
+            nc.gpsimd.tensor_scalar(res[:], vec[:], factor, 0.0, ALU.mult, ALU.add)
+            return res
+
+        neg_tau2 = scaled(tau2_t, -1.0, "neg_tau2")
+        ga15 = scaled(ga_t, 1.5, "ga15")
+        gb2 = scaled(gb_t, 2.0, "gb2")
+        neg_tau4 = scaled(tau4_t, -1.0, "neg_tau4")
+        quarter = held.tile([P, 1], F32, name="quarter")
+        nc.gpsimd.memset(quarter[:], 0.25)
+
+        a_win = [held.tile([P, WIN], F32, name="a_win%d" % t) for t in range(PACK)]
+        b_win = [held.tile([P, WIN], F32, name="b_win%d" % t) for t in range(PACK)]
+        for win in b_win + a_win:
+            nc.vector.memset(win[:, N:WIN], 0.0)
+
+        xs_two = held.tile([P, V], U8, name="xs_two", align_bytes=64)
+        nc.vector.tensor_copy(xs_two[:], xs[:].indirect(two_l[:]))
+        w2_w, w2_s = deal_weight(w2_raw, w2s_raw, "w2")
+        xs_offs_raw = held.tile([P, S], U8, name="xs_offs_raw", align_bytes=64)
+        nc.vector.tensor_copy(xs_offs_raw[:], xs[:].indirect(offs_l[:]))
+        xs_offs = held.tile([P, S], U8, name="xs_offs", align_bytes=64)
+        nc.vector.tensor_copy(xs_offs[:].bitcast(I32), xs_offs_raw[:].bitcast(I32))
+        for j in (0, 1):
+            nc.sync.dma_start(xs_offs[2 + j : P : 32, :].bitcast(I32), xs_offs_raw[16 + j : P : 32, :].bitcast(I32))
+
+        xw_two = held.tile([P, V], U32, name="xw_two", align_bytes=64)
+        nc.vector.tensor_copy(xw_two[:], xw[:].bitcast(U32).indirect(two_l[:]))
+
+        def first_product(words, scales, x_codes, x_sc, name):
+            banks = []
+            for t in range(PACK):
+                bank = psum.tile([P, N], F32, name="%s%d" % (name, t), tag="%s%d" % (name, t))
+                nc.tensor.matmul_mx(
+                    out=bank[:],
+                    lhsT=words[:, 2 * P * t : 2 * P * (t + 1)].bitcast(FP4X4),
+                    lhsT_scale=scales[:, P * t : P * (t + 1)],
+                    rhs=x_codes[:].bitcast(FP8X4),
+                    rhs_scale=x_sc[:],
+                    start=True,
+                    stop=True,
+                )
+                banks.append(bank)
+            return banks
+
+        b_ps = first_product(w2_w, w2_s, xw_two, xs_two, "pb")
+
+        top2 = held.tile([P, PACK], F32, name="top2")
+        bias3 = held.tile([P, PACK], F32, name="bias3")
+        ea3 = held.tile([P, PACK, N], F32, name="ea3")
+
+        def b_stage(t):
+            c = slice(t, t + 1)
+            nc.vector.tensor_scalar(b_win[t][:, 0:N], b_ps[t][:], 1.0, None, ALU.mult, ALU.max, accum_out=top2[:, c])
+            nc.vector.tensor_scalar(bias3[:, c], top2[:, c], tau3_t[:, c], -1.0, ALU.mult, ALU.mult)
+            nc.scalar.activation(ea3[:, t, :], b_win[t][:].indirect(n3_l[:]), ACT.Exp, bias=bias3[:, c], scale=tau3_t[:, c])
+
+        b_stage(0)
+        w1_w, w1_s = deal_weight(w1_raw, w1s_raw, "w1")
+        xw_offs = held.tile([P, S], U32, name="xw_offs", align_bytes=64)
+        nc.vector.tensor_copy(xw_offs[:], xw[:].bitcast(U32).indirect(offs_l[:]))
+        a_ps = first_product(w1_w, w1_s, xw_offs, xs_offs, "pa")
+        b_stage(1)
+
+        top = held.tile([P, PACK], F32, name="top")
+        low = held.tile([P, PACK], F32, name="low")
+        bias1 = held.tile([P, PACK], F32, name="bias1")
+        bias2 = held.tile([P, PACK], F32, name="bias2")
+        z_planes = held.tile([P, PACK, S], BF16, name="z_planes")
+
+        def a_stats(t):
+            c = slice(t, t + 1)
+            nc.vector.tensor_scalar(a_win[t][:, 0:N], a_ps[t][:], 1.0, None, ALU.mult, ALU.max, accum_out=top[:, c])
+            nc.vector.tensor_reduce(low[:, c], a_ps[t][:], AX.X, ALU.min)
+            nc.vector.tensor_scalar(bias1[:, c], top[:, c], tau_t[:, c], -1.0, ALU.mult, ALU.mult)
+            nc.vector.tensor_scalar(bias2[:, c], low[:, c], tau2_t[:, c], 1.0, ALU.mult, ALU.mult)
+
+        def a_exps(t):
+            c = slice(t, t + 1)
+            ea = ring.tile([P, S], F32, name="ea")
+            ea2 = ring.tile([P, S], F32, name="ea2")
+            nc.scalar.activation(ea[:], a_win[t][:].indirect(n1_l[:]), ACT.Exp, bias=bias1[:, c], scale=tau_t[:, c])
+            nc.scalar.activation(ea2[:], a_win[t][:].indirect(n2_l[:]), ACT.Exp, bias=bias2[:, c], scale=neg_tau2[:, c])
+            return ea, ea2
+
+        def a_finish(t, ea, ea2):
+            c = slice(t, t + 1)
+            both = ring.tile([P, S], F32, name="both")
+            nc.vector.tensor_tensor(
+                both[:].rearrange("p (u m) -> p m u", u=PACK),
+                ea[:].rearrange("p (m u) -> p m u", u=PACK),
+                ea2[:].rearrange("p (m u) -> p m u", u=PACK),
+                ALU.add,
+            )
+            nc.vector.scalar_tensor_tensor(
+                z_planes[:, t, :].rearrange("p (u m) -> p u m", u=PACK),
+                a_ps[t][:].rearrange("p (m u) -> p u m", u=PACK),
+                ga15[:, c],
+                both[:].rearrange("p (u m) -> p u m", u=PACK),
+                ALU.mult,
+                ALU.mult,
+            )
+
+        def mx_tiles(name):
+            woven = held.tile([P, N * PACK], BF16, name=name + "_woven", align_bytes=64)
+            codes = held.tile([P, N], U32, name=name + "_codes", align_bytes=64)
+            scales = held.tile([P, N], U8, name=name + "_scales", align_bytes=64)
+            return woven, codes, scales
+
+        def weave(copy, woven, planes, cols):
+            copy(
+                woven[:, PACK * cols.start : PACK * cols.stop].rearrange("p (c i t) -> p c t i", i=4, t=PACK),
+                planes[:, :, cols].rearrange("p t (c i) -> p c t i", i=4),
+            )
+
+        def quantize(woven, codes, scales, cols):
+            nc.vector.quantize_mx(
+                out=codes[:, cols].bitcast(FP8X4), scales=scales[:, cols], in_=woven[:, PACK * cols.start : PACK * cols.stop]
+            )
+
+        whole = slice(0, N)
+        halves = (slice(0, N // 2), slice(N // 2, N))
+
+        a_stats(0)
+        b_stage(2)
+        exps = a_exps(0)
+        a_stats(1)
+        b_stage(3)
+        for t in range(1, PACK):
+            nxt = a_exps(t)
+            if t + 1 < PACK:
+                a_stats(t + 1)
+            a_finish(t - 1, *exps)
+            exps = nxt
+        a_finish(PACK - 1, *exps)
+        z_woven, z_codes, z_scales = mx_tiles("z")
+        weave(nc.vector.tensor_copy, z_woven, z_planes, whole)
+        quantize(z_woven, z_codes, z_scales, whole)
+
+        log_rest = held.tile([P, PACK, V], F32, name="log_rest", tag="a_win3")
+        for t in range(PACK):
+            nc.scalar.activation(log_rest[:, t, :], ea3[:, t, :], ACT.Ln, bias=quarter[:], scale=1.0)
+        logit = held.tile([P, PACK, V], F32, name="logit")
+        share = held.tile([P, PACK, V], F32, name="share")
+        z2_planes = held.tile([P, PACK, V], BF16, name="z2_planes")
+        for t in range(PACK):
+            c = slice(t, t + 1)
+            nc.vector.scalar_tensor_tensor(logit[:, t, :], b_ps[t][:], tau3_t[:, c], log_rest[:, t, :], ALU.mult, ALU.subtract)
+        z2_woven, z2_codes, z2_scales = mx_tiles("z2")
+        s_ps = [psum.tile([P, V], F32, name="ps%d" % t, tag="pa%d" % t) for t in range(PACK)]
+        for cols in halves:
+            for t in range(PACK):
+                c = slice(t, t + 1)
+                nc.scalar.activation(share[:, t, cols], logit[:, t, cols], ACT.Sigmoid, bias=bias3[:, c], scale=1.0)
+                nc.vector.scalar_tensor_tensor(z2_planes[:, t, cols], b_ps[t][:, cols], gb2[:, c], share[:, t, cols], ALU.mult, ALU.mult)
+            weave(nc.vector.tensor_copy, z2_woven, z2_planes, cols)
+            quantize(z2_woven, z2_codes, z2_scales, cols)
+            for t in range(PACK):
+                nc.tensor.matmul_mx(
+                    out=s_ps[t][:, cols],
+                    lhsT=z_codes[:, P * t : P * (t + 1)].bitcast(FP8X4),
+                    lhsT_scale=z_scales[:, P * t : P * (t + 1)],
+                    rhs=z2_codes[:, cols].bitcast(FP8X4),
+                    rhs_scale=z2_scales[:, cols],
+                    start=True,
+                    stop=True,
+                )
+
+        res = held.tile([P, PACK, V], F32, name="res")
+        out_rows = out_0.rearrange("(p t) v -> p t v", t=PACK)
+        o_woven, o_codes, o_scales = mx_tiles("o")
+        out_words = out_1[0].rearrange("p c r -> p (c r)").bitcast(I32)
+        for t in range(PACK):
+            nc.vector.tensor_scalar(b_win[t][:, 0:N], s_ps[t][:], -0.03125, None, ALU.mult)
+        for t in range(PACK):
+            c = slice(t, t + 1)
+            sq_win = a_win[t % 3]
+            nc.scalar.activation(sq_win[:, 0:N], s_ps[t][:], ACT.Square, scale=0.0625)
+            ea4 = ring.tile([P, V], F32, name="ea")
+            prod = ring.tile([P, V], F32, name="both")
+            for cols in halves if t == PACK - 1 else (whole,):
+                entries = slice(cols.start // 16, cols.stop // 16)
+                nc.scalar.activation(ea4[:, cols], sq_win[:].indirect(n4_l[:, entries]), ACT.Exp, scale=neg_tau4[:, c])
+                nc.vector.scalar_tensor_tensor(prod[:, cols], s_ps[t][:, cols], 0.0625, ea4[:, cols], ALU.mult, ALU.mult)
+                nc.vector.tensor_tensor(res[:, t, cols], b_win[t][:].indirect(n5_l[:, entries]), prod[:, cols], ALU.add)
+                nc.sync.dma_start(out_rows[:, t, cols], res[:, t, cols])
+        weave(nc.scalar.copy, o_woven, res, halves[0])
+        weave(nc.vector.tensor_copy, o_woven, res, halves[1])
+        for cols in reversed(halves):
+            quantize(o_woven, o_codes, o_scales, cols)
+            nc.sync.dma_start(out_words[:, cols], o_codes[:, cols].bitcast(I32))
+        sc_rows = out_2[0].bitcast(I32)
+        for q in range(4):
+            nc.scalar.dma_start(sc_rows[4 * q : 4 * q + 4, :], o_scales[32 * q : 32 * q + 4, :].bitcast(I32))

@@ -21,6 +21,7 @@ P = 128
 PACK = 4
 N = 512
 WIN = 1024
+XW_FIRST = 512
 
 
 def tile_picked_hkqedfeshega_none_po_kernel(
@@ -31,7 +32,7 @@ def tile_picked_hkqedfeshega_none_po_kernel(
     nc = tc.nc
     with ExitStack() as ctx:
         held = ctx.enter_context(tc.tile_pool(name="held", bufs=1))
-        ring = ctx.enter_context(tc.tile_pool(name="ring", bufs=2))
+        ring = ctx.enter_context(tc.tile_pool(name="ring", bufs=4))
         psum = ctx.enter_context(tc.psum_pool(name="psum", bufs=1))
 
         def load_list(src, name):
@@ -39,13 +40,13 @@ def tile_picked_hkqedfeshega_none_po_kernel(
             nc.sync.dma_start(lst[:], src)
             return lst
 
-        def load_rows(src, name):
+        def load_rows(queue, src, name):
             vec = held.tile([P, PACK], F32, name=name)
-            nc.gpsimd.dma_start(vec[:], src.rearrange("(p t) o -> p (t o)", t=PACK))
+            queue.dma_start(vec[:], src.rearrange("(p t) o -> p (t o)", t=PACK))
             return vec
 
         def cleared_bytes(width, name):
-            raw = held.tile([P, width], U8, name=name)
+            raw = held.tile([P, width], U8, name=name, align_bytes=64)
             nc.gpsimd.memset(raw[:].bitcast(I32), 0)
             return raw
 
@@ -54,16 +55,16 @@ def tile_picked_hkqedfeshega_none_po_kernel(
             for q in range(4):
                 queues[q].dma_start(raw[32 * q : 32 * q + 4, :].bitcast(I32), rows[4 * q : 4 * q + 4, :])
 
-        def deal_weight(raw_words, raw_scales, name):
+        def deal_weight(byte_engine, raw_words, raw_scales, name):
             words = held.tile([P, 2 * H], U8, name=name + "_words", align_bytes=64)
             scales = held.tile([P, H], U8, name=name + "_scales", align_bytes=64)
             nc.scalar.copy(
                 words[:].bitcast(U16).rearrange("p (t m) -> p m t", t=PACK),
                 raw_words[:].bitcast(U16).rearrange("p (m t) -> p m t", t=PACK),
             )
-            nc.vector.tensor_copy(
-                scales[:].rearrange("p (t m) -> p m t", t=PACK),
-                raw_scales[:].rearrange("p (m t) -> p m t", t=PACK),
+            byte_engine.tensor_copy(
+                scales[:].rearrange("p (t m) -> p t m", t=PACK),
+                raw_scales[:].rearrange("p (m t) -> p t m", t=PACK),
             )
             return words, scales
 
@@ -71,10 +72,9 @@ def tile_picked_hkqedfeshega_none_po_kernel(
         w2s_raw = cleared_bytes(H, "w2s_raw")
         w1s_raw = cleared_bytes(H, "w1s_raw")
         two_l = load_list(two, "two_l")
-        offs_l = load_list(offs, "offs_l")
-        n3_l = load_list(n3, "n3_l")
         xw = held.tile([P, T], I32, name="xw")
-        nc.sync.dma_start(xw[:], x_words[0].rearrange("p n r -> p (n r)").bitcast(I32))
+        xw_src = x_words[0].rearrange("p n r -> p (n r)").bitcast(I32)
+        nc.sync.dma_start(xw[:, 0:XW_FIRST], xw_src[:, 0:XW_FIRST])
         xs_rows = x_scales[0].bitcast(I32)
         by2 = xs_rows.rearrange("(r j) c -> j r c", j=2)
         by4 = xs_rows.rearrange("(q j) c -> j q c", j=4)
@@ -82,22 +82,22 @@ def tile_picked_hkqedfeshega_none_po_kernel(
             nc.sync.dma_start(xs[j:P:16, :].bitcast(I32), by2[j])
         for j in (2, 3):
             nc.sync.dma_start(xs[j:P:32, :].bitcast(I32), by4[j])
+        offs_l = load_list(offs, "offs_l")
+        nc.sync.dma_start(xw[:, XW_FIRST:T], xw_src[:, XW_FIRST:T])
         w2_raw = held.tile([P, 2 * H], U8, name="w2_raw")
         nc.sync.dma_start(w2_raw[:].bitcast(I32), w2_words[0].bitcast(I32))
-        load_weight_scales((nc.sync, nc.sync, nc.gpsimd, nc.gpsimd), w2s_raw, w2_scales)
-        tau3_t = load_rows(tau3, "tau3_t")
+        load_weight_scales((nc.sync,) * 4, w2s_raw, w2_scales)
+        tau3_t = load_rows(nc.gpsimd, tau3, "tau3_t")
+        n3_l = load_list(n3, "n3_l")
         w1_raw = held.tile([P, 2 * H], U8, name="w1_raw")
         nc.sync.dma_start(w1_raw[:].bitcast(I32), w1_words[0].bitcast(I32))
         load_weight_scales((nc.sync,) * 4, w1s_raw, w1_scales)
-        tau_t = load_rows(tau, "tau_t")
-        tau2_t = load_rows(tau2, "tau2_t")
+        tau_t = load_rows(nc.gpsimd, tau, "tau_t")
+        tau2_t = load_rows(nc.gpsimd, tau2, "tau2_t")
         n1_l = load_list(n1, "n1_l")
         n2_l = load_list(n2, "n2_l")
         n4_l = load_list(n4, "n4_l")
         n5_l = load_list(n5, "n5_l")
-        ga_t = load_rows(ga, "ga_t")
-        gb_t = load_rows(gb, "gb_t")
-        tau4_t = load_rows(tau4, "tau4_t")
 
         def scaled(vec, factor, name):
             res = held.tile([P, PACK], F32, name=name)
@@ -105,29 +105,27 @@ def tile_picked_hkqedfeshega_none_po_kernel(
             return res
 
         neg_tau2 = scaled(tau2_t, -1.0, "neg_tau2")
-        ga15 = scaled(ga_t, 1.5, "ga15")
-        gb2 = scaled(gb_t, 2.0, "gb2")
-        neg_tau4 = scaled(tau4_t, -1.0, "neg_tau4")
         quarter = held.tile([P, 1], F32, name="quarter")
         nc.gpsimd.memset(quarter[:], 0.25)
 
-        a_win = [held.tile([P, WIN], F32, name="a_win%d" % t) for t in range(PACK)]
-        b_win = [held.tile([P, WIN], F32, name="b_win%d" % t) for t in range(PACK)]
-        for win in b_win + a_win:
+        wins = [held.tile([P, WIN], F32, name="win%d" % t) for t in range(PACK)]
+        for win in wins:
             nc.vector.memset(win[:, N:WIN], 0.0)
+        a_win = wins
+        b_win = wins
 
         xs_two = held.tile([P, V], U8, name="xs_two", align_bytes=64)
         nc.vector.tensor_copy(xs_two[:], xs[:].indirect(two_l[:]))
-        w2_w, w2_s = deal_weight(w2_raw, w2s_raw, "w2")
-        xs_offs_raw = held.tile([P, S], U8, name="xs_offs_raw", align_bytes=64)
+        xw_two = held.tile([P, V], U32, name="xw_two", align_bytes=64)
+        nc.vector.tensor_copy(xw_two[:], xw[:].bitcast(U32).indirect(two_l[:]))
+        w2_w, w2_s = deal_weight(nc.vector, w2_raw, w2s_raw, "w2")
+        xs_offs_raw = held.tile([P, S], U8, name="xs_offs_raw", tag="w2s_raw", align_bytes=64)
         nc.vector.tensor_copy(xs_offs_raw[:], xs[:].indirect(offs_l[:]))
         xs_offs = held.tile([P, S], U8, name="xs_offs", align_bytes=64)
         nc.vector.tensor_copy(xs_offs[:].bitcast(I32), xs_offs_raw[:].bitcast(I32))
         for j in (0, 1):
             nc.sync.dma_start(xs_offs[2 + j : P : 32, :].bitcast(I32), xs_offs_raw[16 + j : P : 32, :].bitcast(I32))
 
-        xw_two = held.tile([P, V], U32, name="xw_two", align_bytes=64)
-        nc.vector.tensor_copy(xw_two[:], xw[:].bitcast(U32).indirect(two_l[:]))
 
         def first_product(words, scales, x_codes, x_sc, name):
             banks = []
@@ -149,20 +147,28 @@ def tile_picked_hkqedfeshega_none_po_kernel(
 
         top2 = held.tile([P, PACK], F32, name="top2")
         bias3 = held.tile([P, PACK], F32, name="bias3")
-        ea3 = held.tile([P, PACK, N], F32, name="ea3")
+        ea3 = held.tile([P, PACK * N], F32, name="ea3")
 
         def b_stage(t):
             c = slice(t, t + 1)
             nc.vector.tensor_scalar(b_win[t][:, 0:N], b_ps[t][:], 1.0, None, ALU.mult, ALU.max, accum_out=top2[:, c])
             nc.vector.tensor_scalar(bias3[:, c], top2[:, c], tau3_t[:, c], -1.0, ALU.mult, ALU.mult)
-            nc.scalar.activation(ea3[:, t, :], b_win[t][:].indirect(n3_l[:]), ACT.Exp, bias=bias3[:, c], scale=tau3_t[:, c])
+            nc.scalar.activation(ea3[:, N * t : N * (t + 1)], b_win[t][:].indirect(n3_l[:]), ACT.Exp, bias=bias3[:, c], scale=tau3_t[:, c])
 
         b_stage(0)
-        w1_w, w1_s = deal_weight(w1_raw, w1s_raw, "w1")
-        xw_offs = held.tile([P, S], U32, name="xw_offs", align_bytes=64)
+        b_stage(1)
+        w1_w, w1_s = deal_weight(nc.gpsimd, w1_raw, w1s_raw, "w1")
+        xw_offs = held.tile([P, S], U32, name="xw_offs", tag="xw_two", align_bytes=64)
         nc.vector.tensor_copy(xw_offs[:], xw[:].bitcast(U32).indirect(offs_l[:]))
         a_ps = first_product(w1_w, w1_s, xw_offs, xs_offs, "pa")
-        b_stage(1)
+
+        ga_t = load_rows(nc.sync, ga, "ga_t")
+        gb_t = load_rows(nc.sync, gb, "gb_t")
+        tau4_t = load_rows(nc.sync, tau4, "tau4_t")
+
+        ga15 = scaled(ga_t, 1.5, "ga15")
+        gb2 = scaled(gb_t, 2.0, "gb2")
+        neg_tau4 = scaled(tau4_t, -1.0, "neg_tau4")
 
         top = held.tile([P, PACK], F32, name="top")
         low = held.tile([P, PACK], F32, name="low")
@@ -223,31 +229,27 @@ def tile_picked_hkqedfeshega_none_po_kernel(
         whole = slice(0, N)
         halves = (slice(0, N // 2), slice(N // 2, N))
 
-        a_stats(0)
         b_stage(2)
-        exps = a_exps(0)
-        a_stats(1)
         b_stage(3)
-        for t in range(1, PACK):
-            nxt = a_exps(t)
-            if t + 1 < PACK:
-                a_stats(t + 1)
-            a_finish(t - 1, *exps)
-            exps = nxt
-        a_finish(PACK - 1, *exps)
+        for t in range(PACK):
+            a_stats(t)
+        for t in range(PACK):
+            a_finish(t, *a_exps(t))
         z_woven, z_codes, z_scales = mx_tiles("z")
         weave(nc.vector.tensor_copy, z_woven, z_planes, whole)
         quantize(z_woven, z_codes, z_scales, whole)
 
-        log_rest = held.tile([P, PACK, V], F32, name="log_rest", tag="a_win3")
+        log_rest = [wins[3][:, 0:N], wins[3][:, N:WIN], ea3[:, 0:N], ea3[:, N : 2 * N]]
         for t in range(PACK):
-            nc.scalar.activation(log_rest[:, t, :], ea3[:, t, :], ACT.Ln, bias=quarter[:], scale=1.0)
-        logit = held.tile([P, PACK, V], F32, name="logit")
-        share = held.tile([P, PACK, V], F32, name="share")
+            nc.scalar.activation(log_rest[t], ea3[:, N * t : N * (t + 1)], ACT.Ln, bias=quarter[:], scale=1.0)
+        logit_flat = held.tile([P, PACK * V], F32, name="logit")
+        share_flat = held.tile([P, PACK * V], F32, name="share")
+        logit = logit_flat[:].rearrange("p (t v) -> p t v", t=PACK)
+        share = share_flat[:].rearrange("p (t v) -> p t v", t=PACK)
         z2_planes = held.tile([P, PACK, V], BF16, name="z2_planes")
         for t in range(PACK):
             c = slice(t, t + 1)
-            nc.vector.scalar_tensor_tensor(logit[:, t, :], b_ps[t][:], tau3_t[:, c], log_rest[:, t, :], ALU.mult, ALU.subtract)
+            nc.vector.scalar_tensor_tensor(logit[:, t, :], b_ps[t][:], tau3_t[:, c], log_rest[t], ALU.mult, ALU.subtract)
         z2_woven, z2_codes, z2_scales = mx_tiles("z2")
         s_ps = [psum.tile([P, V], F32, name="ps%d" % t, tag="pa%d" % t) for t in range(PACK)]
         for cols in halves:
@@ -272,19 +274,22 @@ def tile_picked_hkqedfeshega_none_po_kernel(
         out_rows = out_0.rearrange("(p t) v -> p t v", t=PACK)
         o_woven, o_codes, o_scales = mx_tiles("o")
         out_words = out_1[0].rearrange("p c r -> p (c r)").bitcast(I32)
-        for t in range(PACK):
-            nc.vector.tensor_scalar(b_win[t][:, 0:N], s_ps[t][:], -0.03125, None, ALU.mult)
+        half_win = [logit_flat, share_flat, ea3, wins[3]]
+        for t in range(2):
+            nc.vector.tensor_scalar(half_win[t][:, 0:N], s_ps[t][:], -0.03125, None, ALU.mult)
         for t in range(PACK):
             c = slice(t, t + 1)
             sq_win = a_win[t % 3]
             nc.scalar.activation(sq_win[:, 0:N], s_ps[t][:], ACT.Square, scale=0.0625)
+            if t >= 2:
+                nc.scalar.activation(half_win[t][:, 0:N], s_ps[t][:], ACT.Copy, scale=-0.03125)
             ea4 = ring.tile([P, V], F32, name="ea")
             prod = ring.tile([P, V], F32, name="both")
             for cols in halves if t == PACK - 1 else (whole,):
                 entries = slice(cols.start // 16, cols.stop // 16)
                 nc.scalar.activation(ea4[:, cols], sq_win[:].indirect(n4_l[:, entries]), ACT.Exp, scale=neg_tau4[:, c])
                 nc.vector.scalar_tensor_tensor(prod[:, cols], s_ps[t][:, cols], 0.0625, ea4[:, cols], ALU.mult, ALU.mult)
-                nc.vector.tensor_tensor(res[:, t, cols], b_win[t][:].indirect(n5_l[:, entries]), prod[:, cols], ALU.add)
+                nc.vector.tensor_tensor(res[:, t, cols], half_win[t][:].indirect(n5_l[:, entries]), prod[:, cols], ALU.add)
                 nc.sync.dma_start(out_rows[:, t, cols], res[:, t, cols])
         weave(nc.scalar.copy, o_woven, res, halves[0])
         weave(nc.vector.tensor_copy, o_woven, res, halves[1])

@@ -22,6 +22,7 @@ PACK = 4
 N = 512
 WIN = 1024
 XW_FIRST = 512
+SCALAR_WEAVE = 192
 
 
 def tile_picked_hkqedfeshega_none_po_kernel(
@@ -237,7 +238,6 @@ def tile_picked_hkqedfeshega_none_po_kernel(
             a_finish(t, *a_exps(t))
         z_woven, z_codes, z_scales = mx_tiles("z")
         weave(nc.vector.tensor_copy, z_woven, z_planes, whole)
-        quantize(z_woven, z_codes, z_scales, whole)
 
         log_rest = [wins[3][:, 0:N], wins[3][:, N:WIN], ea3[:, 0:N], ea3[:, N : 2 * N]]
         for t in range(PACK):
@@ -250,52 +250,82 @@ def tile_picked_hkqedfeshega_none_po_kernel(
         for t in range(PACK):
             c = slice(t, t + 1)
             nc.vector.scalar_tensor_tensor(logit[:, t, :], b_ps[t][:], tau3_t[:, c], log_rest[t], ALU.mult, ALU.subtract)
+        quantize(z_woven, z_codes, z_scales, whole)
         z2_woven, z2_codes, z2_scales = mx_tiles("z2")
-        s_ps = [psum.tile([P, V], F32, name="ps%d" % t, tag="pa%d" % t) for t in range(PACK)]
-        for cols in halves:
-            for t in range(PACK):
-                c = slice(t, t + 1)
+        for t in range(PACK):
+            c = slice(t, t + 1)
+            for cols in halves if t == PACK - 1 else (whole,):
                 nc.scalar.activation(share[:, t, cols], logit[:, t, cols], ACT.Sigmoid, bias=bias3[:, c], scale=1.0)
                 nc.vector.scalar_tensor_tensor(z2_planes[:, t, cols], b_ps[t][:, cols], gb2[:, c], share[:, t, cols], ALU.mult, ALU.mult)
-            weave(nc.vector.tensor_copy, z2_woven, z2_planes, cols)
-            quantize(z2_woven, z2_codes, z2_scales, cols)
-            for t in range(PACK):
-                nc.tensor.matmul_mx(
-                    out=s_ps[t][:, cols],
-                    lhsT=z_codes[:, P * t : P * (t + 1)].bitcast(FP8X4),
-                    lhsT_scale=z_scales[:, P * t : P * (t + 1)],
-                    rhs=z2_codes[:, cols].bitcast(FP8X4),
-                    rhs_scale=z2_scales[:, cols],
-                    start=True,
-                    stop=True,
-                )
+        weave(nc.scalar.copy, z2_woven, z2_planes, slice(0, SCALAR_WEAVE))
+        warm = held.tile([P, 1], F32, name="warm")
+        nc.scalar.activation(warm[:], z2_woven[:, 0:1], ACT.Exp, scale=0.0)
+        weave(nc.vector.tensor_copy, z2_woven, z2_planes, slice(SCALAR_WEAVE, N))
+        quantize(z2_woven, z2_codes, z2_scales, whole)
+        s_ps = []
+        for t in range(PACK):
+            bank = psum.tile([P, V], F32, name="ps%d" % t, tag="pa%d" % t)
+            nc.tensor.matmul_mx(
+                out=bank[:],
+                lhsT=z_codes[:, P * t : P * (t + 1)].bitcast(FP8X4),
+                lhsT_scale=z_scales[:, P * t : P * (t + 1)],
+                rhs=z2_codes[:].bitcast(FP8X4),
+                rhs_scale=z2_scales[:],
+                start=True,
+                stop=True,
+            )
+            s_ps.append(bank)
 
         res = held.tile([P, PACK, V], F32, name="res")
         out_rows = out_0.rearrange("(p t) v -> p t v", t=PACK)
         o_woven, o_codes, o_scales = mx_tiles("o")
-        out_words = out_1[0].rearrange("p c r -> p (c r)").bitcast(I32)
-        half_win = [logit_flat, share_flat, ea3, wins[3]]
+        half_win = [logit_flat, share_flat, wins[1], wins[2]]
+        sq_win = [wins[0], wins[1], wins[0], wins[0]]
+        ea4 = [wins[2][:, 0:N], ea3[:, 0:N], ea3[:, N : 2 * N], ea3[:, 2 * N : 3 * N]]
+
+        def square(t):
+            nc.scalar.activation(sq_win[t][:, 0:N], s_ps[t][:], ACT.Square, scale=0.0625)
+
+        def halve(t):
+            nc.scalar.activation(half_win[t][:, 0:N], s_ps[t][:], ACT.Copy, scale=-0.03125)
+
+        def decay(t, cols):
+            entries = slice(cols.start // 16, cols.stop // 16)
+            nc.scalar.activation(ea4[t][:, cols], sq_win[t][:].indirect(n4_l[:, entries]), ACT.Exp, scale=neg_tau4[:, t : t + 1])
+
+        def product(t, cols):
+            prod = ring.tile([P, cols.stop - cols.start], F32, name="both")
+            nc.vector.scalar_tensor_tensor(prod[:], s_ps[t][:, cols], 0.0625, ea4[t][:, cols], ALU.mult, ALU.mult)
+            return prod
+
+        def finish(t, cols=whole):
+            entries = slice(cols.start // 16, cols.stop // 16)
+            prod = product(t, cols)
+            nc.vector.tensor_tensor(res[:, t, cols], half_win[t][:].indirect(n5_l[:, entries]), prod[:], ALU.add)
+            nc.sync.dma_start(out_rows[:, t, cols], res[:, t, cols])
+
+        square(0)
         for t in range(2):
             nc.vector.tensor_scalar(half_win[t][:, 0:N], s_ps[t][:], -0.03125, None, ALU.mult)
-        for t in range(PACK):
-            c = slice(t, t + 1)
-            sq_win = a_win[t % 3]
-            nc.scalar.activation(sq_win[:, 0:N], s_ps[t][:], ACT.Square, scale=0.0625)
-            if t >= 2:
-                nc.scalar.activation(half_win[t][:, 0:N], s_ps[t][:], ACT.Copy, scale=-0.03125)
-            ea4 = ring.tile([P, V], F32, name="ea")
-            prod = ring.tile([P, V], F32, name="both")
-            for cols in halves if t == PACK - 1 else (whole,):
-                entries = slice(cols.start // 16, cols.stop // 16)
-                nc.scalar.activation(ea4[:, cols], sq_win[:].indirect(n4_l[:, entries]), ACT.Exp, scale=neg_tau4[:, c])
-                nc.vector.scalar_tensor_tensor(prod[:, cols], s_ps[t][:, cols], 0.0625, ea4[:, cols], ALU.mult, ALU.mult)
-                nc.vector.tensor_tensor(res[:, t, cols], half_win[t][:].indirect(n5_l[:, entries]), prod[:, cols], ALU.add)
-                nc.sync.dma_start(out_rows[:, t, cols], res[:, t, cols])
+        nc.vector.scalar_tensor_tensor(sq_win[1][:, 0:N], s_ps[1][:], -0.125, half_win[1][:, 0:N], ALU.mult, ALU.mult)
+        decay(0, whole)
+        decay(1, whole)
+        finish(0)
+        square(2)
+        halve(2)
+        decay(2, whole)
+        finish(1)
+        square(3)
+        halve(3)
+        for cols in halves:
+            decay(3, cols)
+        finish(2)
+        for cols in halves:
+            finish(3, cols)
         weave(nc.scalar.copy, o_woven, res, halves[0])
         weave(nc.vector.tensor_copy, o_woven, res, halves[1])
-        for cols in reversed(halves):
-            quantize(o_woven, o_codes, o_scales, cols)
-            nc.sync.dma_start(out_words[:, cols], o_codes[:, cols].bitcast(I32))
+        quantize(o_woven, o_codes, o_scales, whole)
+        nc.sync.dma_start(out_1[0].rearrange("p c r -> p (c r)").bitcast(I32), o_codes[:].bitcast(I32))
         sc_rows = out_2[0].bitcast(I32)
         for q in range(4):
-            nc.scalar.dma_start(sc_rows[4 * q : 4 * q + 4, :], o_scales[32 * q : 32 * q + 4, :].bitcast(I32))
+            (nc.scalar, nc.sync)[q % 2].dma_start(sc_rows[4 * q : 4 * q + 4, :], o_scales[32 * q : 32 * q + 4, :].bitcast(I32))

@@ -2,8 +2,9 @@ from contextlib import ExitStack
 
 import concourse.mybir as mybir
 
-K, T, S, V, H = 512, 2048, 512, 512, 512
-FLOPS = 3 * 2 * 512 * 512 * 512
+T = 2048
+N = 512
+FLOPS = 3 * 2 * N * N * N
 
 F32 = mybir.dt.float32
 BF16 = mybir.dt.bfloat16
@@ -19,10 +20,15 @@ AX = mybir.AxisListType
 
 P = 128
 PACK = 4
-N = 512
-WIN = 1024
-XW_FIRST = 512
-SCALAR_WEAVE = 192
+QUADS = 4
+GROUP = 16
+LAST = PACK - 1
+WINDOW = 2 * N
+X_FIRST = 512
+Z2_SCALAR_COLUMNS = 192
+
+WHOLE = slice(0, N)
+HALVES = (slice(0, N // 2), slice(N // 2, N))
 
 
 def tile_picked_hkqedfeshega_none_po_kernel(
@@ -33,11 +39,11 @@ def tile_picked_hkqedfeshega_none_po_kernel(
     nc = tc.nc
     with ExitStack() as ctx:
         held = ctx.enter_context(tc.tile_pool(name="held", bufs=1))
-        ring = ctx.enter_context(tc.tile_pool(name="ring", bufs=4))
+        ring = ctx.enter_context(tc.tile_pool(name="ring", bufs=PACK))
         psum = ctx.enter_context(tc.psum_pool(name="psum", bufs=1))
 
         def load_list(src, name):
-            lst = held.tile([P, N // 16], U16, name=name)
+            lst = held.tile([P, N // GROUP], U16, name=name)
             nc.sync.dma_start(lst[:], src)
             return lst
 
@@ -46,19 +52,29 @@ def tile_picked_hkqedfeshega_none_po_kernel(
             queue.dma_start(vec[:], src.rearrange("(p t) o -> p (t o)", t=PACK))
             return vec
 
+        def scaled(vec, factor, name):
+            product = held.tile([P, PACK], F32, name=name)
+            nc.gpsimd.tensor_scalar(product[:], vec[:], factor, 0.0, ALU.mult, ALU.add)
+            return product
+
         def cleared_bytes(width, name):
             raw = held.tile([P, width], U8, name=name, align_bytes=64)
             nc.gpsimd.memset(raw[:].bitcast(I32), 0)
             return raw
 
-        def load_weight_scales(queues, raw, src):
+        def load_weight_words(src, name):
+            raw = held.tile([P, 2 * N], U8, name=name)
+            nc.sync.dma_start(raw[:].bitcast(I32), src[0].bitcast(I32))
+            return raw
+
+        def load_weight_scales(raw, src):
             rows = src[0].bitcast(I32)
-            for q in range(4):
-                queues[q].dma_start(raw[32 * q : 32 * q + 4, :].bitcast(I32), rows[4 * q : 4 * q + 4, :])
+            for q in range(QUADS):
+                nc.sync.dma_start(raw[32 * q : 32 * q + 4, :].bitcast(I32), rows[4 * q : 4 * q + 4, :])
 
         def deal_weight(byte_engine, raw_words, raw_scales, name):
-            words = held.tile([P, 2 * H], U8, name=name + "_words", align_bytes=64)
-            scales = held.tile([P, H], U8, name=name + "_scales", align_bytes=64)
+            words = held.tile([P, 2 * N], U8, name=name + "_words", align_bytes=64)
+            scales = held.tile([P, N], U8, name=name + "_scales", align_bytes=64)
             nc.scalar.copy(
                 words[:].bitcast(U16).rearrange("p (t m) -> p m t", t=PACK),
                 raw_words[:].bitcast(U16).rearrange("p (m t) -> p m t", t=PACK),
@@ -69,146 +85,22 @@ def tile_picked_hkqedfeshega_none_po_kernel(
             )
             return words, scales
 
-        xs = cleared_bytes(T, "xs")
-        w2s_raw = cleared_bytes(H, "w2s_raw")
-        w1s_raw = cleared_bytes(H, "w1s_raw")
-        two_l = load_list(two, "two_l")
-        xw = held.tile([P, T], I32, name="xw")
-        xw_src = x_words[0].rearrange("p n r -> p (n r)").bitcast(I32)
-        nc.sync.dma_start(xw[:, 0:XW_FIRST], xw_src[:, 0:XW_FIRST])
-        xs_rows = x_scales[0].bitcast(I32)
-        by2 = xs_rows.rearrange("(r j) c -> j r c", j=2)
-        by4 = xs_rows.rearrange("(q j) c -> j q c", j=4)
-        for j in (0, 1):
-            nc.sync.dma_start(xs[j:P:16, :].bitcast(I32), by2[j])
-        for j in (2, 3):
-            nc.sync.dma_start(xs[j:P:32, :].bitcast(I32), by4[j])
-        offs_l = load_list(offs, "offs_l")
-        nc.sync.dma_start(xw[:, XW_FIRST:T], xw_src[:, XW_FIRST:T])
-        w2_raw = held.tile([P, 2 * H], U8, name="w2_raw")
-        nc.sync.dma_start(w2_raw[:].bitcast(I32), w2_words[0].bitcast(I32))
-        load_weight_scales((nc.sync,) * 4, w2s_raw, w2_scales)
-        tau3_t = load_rows(nc.gpsimd, tau3, "tau3_t")
-        n3_l = load_list(n3, "n3_l")
-        w1_raw = held.tile([P, 2 * H], U8, name="w1_raw")
-        nc.sync.dma_start(w1_raw[:].bitcast(I32), w1_words[0].bitcast(I32))
-        load_weight_scales((nc.sync,) * 4, w1s_raw, w1_scales)
-        tau_t = load_rows(nc.gpsimd, tau, "tau_t")
-        tau2_t = load_rows(nc.gpsimd, tau2, "tau2_t")
-        n1_l = load_list(n1, "n1_l")
-        n2_l = load_list(n2, "n2_l")
-        n4_l = load_list(n4, "n4_l")
-        n5_l = load_list(n5, "n5_l")
-
-        def scaled(vec, factor, name):
-            res = held.tile([P, PACK], F32, name=name)
-            nc.gpsimd.tensor_scalar(res[:], vec[:], factor, 0.0, ALU.mult, ALU.add)
-            return res
-
-        neg_tau2 = scaled(tau2_t, -1.0, "neg_tau2")
-        quarter = held.tile([P, 1], F32, name="quarter")
-        nc.gpsimd.memset(quarter[:], 0.25)
-
-        wins = [held.tile([P, WIN], F32, name="win%d" % t) for t in range(PACK)]
-        for win in wins:
-            nc.vector.memset(win[:, N:WIN], 0.0)
-        a_win = wins
-        b_win = wins
-
-        xs_two = held.tile([P, V], U8, name="xs_two", align_bytes=64)
-        nc.vector.tensor_copy(xs_two[:], xs[:].indirect(two_l[:]))
-        xw_two = held.tile([P, V], U32, name="xw_two", align_bytes=64)
-        nc.vector.tensor_copy(xw_two[:], xw[:].bitcast(U32).indirect(two_l[:]))
-        w2_w, w2_s = deal_weight(nc.vector, w2_raw, w2s_raw, "w2")
-        xs_offs_raw = held.tile([P, S], U8, name="xs_offs_raw", tag="w2s_raw", align_bytes=64)
-        nc.vector.tensor_copy(xs_offs_raw[:], xs[:].indirect(offs_l[:]))
-        xs_offs = held.tile([P, S], U8, name="xs_offs", align_bytes=64)
-        nc.vector.tensor_copy(xs_offs[:].bitcast(I32), xs_offs_raw[:].bitcast(I32))
-        for j in (0, 1):
-            nc.sync.dma_start(xs_offs[2 + j : P : 32, :].bitcast(I32), xs_offs_raw[16 + j : P : 32, :].bitcast(I32))
-
-
-        def first_product(words, scales, x_codes, x_sc, name):
-            banks = []
+        def product(stationary, stationary_dtype, stationary_scales, moving, moving_scales, name, banks):
+            width = stationary.shape[1] // PACK
+            tiles = []
             for t in range(PACK):
-                bank = psum.tile([P, N], F32, name="%s%d" % (name, t), tag="%s%d" % (name, t))
+                bank = psum.tile([P, N], F32, name="%s%d" % (name, t), tag="%s%d" % (banks, t))
                 nc.tensor.matmul_mx(
                     out=bank[:],
-                    lhsT=words[:, 2 * P * t : 2 * P * (t + 1)].bitcast(FP4X4),
-                    lhsT_scale=scales[:, P * t : P * (t + 1)],
-                    rhs=x_codes[:].bitcast(FP8X4),
-                    rhs_scale=x_sc[:],
+                    lhsT=stationary[:, width * t : width * (t + 1)].bitcast(stationary_dtype),
+                    lhsT_scale=stationary_scales[:, P * t : P * (t + 1)],
+                    rhs=moving[:].bitcast(FP8X4),
+                    rhs_scale=moving_scales[:],
                     start=True,
                     stop=True,
                 )
-                banks.append(bank)
-            return banks
-
-        b_ps = first_product(w2_w, w2_s, xw_two, xs_two, "pb")
-
-        top2 = held.tile([P, PACK], F32, name="top2")
-        bias3 = held.tile([P, PACK], F32, name="bias3")
-        ea3 = held.tile([P, PACK * N], F32, name="ea3")
-
-        def b_stage(t):
-            c = slice(t, t + 1)
-            nc.vector.tensor_scalar(b_win[t][:, 0:N], b_ps[t][:], 1.0, None, ALU.mult, ALU.max, accum_out=top2[:, c])
-            nc.vector.tensor_scalar(bias3[:, c], top2[:, c], tau3_t[:, c], -1.0, ALU.mult, ALU.mult)
-            nc.scalar.activation(ea3[:, N * t : N * (t + 1)], b_win[t][:].indirect(n3_l[:]), ACT.Exp, bias=bias3[:, c], scale=tau3_t[:, c])
-
-        b_stage(0)
-        b_stage(1)
-        w1_w, w1_s = deal_weight(nc.gpsimd, w1_raw, w1s_raw, "w1")
-        xw_offs = held.tile([P, S], U32, name="xw_offs", tag="xw_two", align_bytes=64)
-        nc.vector.tensor_copy(xw_offs[:], xw[:].bitcast(U32).indirect(offs_l[:]))
-        a_ps = first_product(w1_w, w1_s, xw_offs, xs_offs, "pa")
-
-        ga_t = load_rows(nc.sync, ga, "ga_t")
-        gb_t = load_rows(nc.sync, gb, "gb_t")
-        tau4_t = load_rows(nc.sync, tau4, "tau4_t")
-
-        ga15 = scaled(ga_t, 1.5, "ga15")
-        gb2 = scaled(gb_t, 2.0, "gb2")
-        neg_tau4 = scaled(tau4_t, -1.0, "neg_tau4")
-
-        top = held.tile([P, PACK], F32, name="top")
-        low = held.tile([P, PACK], F32, name="low")
-        bias1 = held.tile([P, PACK], F32, name="bias1")
-        bias2 = held.tile([P, PACK], F32, name="bias2")
-        z_planes = held.tile([P, PACK, S], BF16, name="z_planes")
-
-        def a_stats(t):
-            c = slice(t, t + 1)
-            nc.vector.tensor_scalar(a_win[t][:, 0:N], a_ps[t][:], 1.0, None, ALU.mult, ALU.max, accum_out=top[:, c])
-            nc.vector.tensor_reduce(low[:, c], a_ps[t][:], AX.X, ALU.min)
-            nc.vector.tensor_scalar(bias1[:, c], top[:, c], tau_t[:, c], -1.0, ALU.mult, ALU.mult)
-            nc.vector.tensor_scalar(bias2[:, c], low[:, c], tau2_t[:, c], 1.0, ALU.mult, ALU.mult)
-
-        def a_exps(t):
-            c = slice(t, t + 1)
-            ea = ring.tile([P, S], F32, name="ea")
-            ea2 = ring.tile([P, S], F32, name="ea2")
-            nc.scalar.activation(ea[:], a_win[t][:].indirect(n1_l[:]), ACT.Exp, bias=bias1[:, c], scale=tau_t[:, c])
-            nc.scalar.activation(ea2[:], a_win[t][:].indirect(n2_l[:]), ACT.Exp, bias=bias2[:, c], scale=neg_tau2[:, c])
-            return ea, ea2
-
-        def a_finish(t, ea, ea2):
-            c = slice(t, t + 1)
-            both = ring.tile([P, S], F32, name="both")
-            nc.vector.tensor_tensor(
-                both[:].rearrange("p (u m) -> p m u", u=PACK),
-                ea[:].rearrange("p (m u) -> p m u", u=PACK),
-                ea2[:].rearrange("p (m u) -> p m u", u=PACK),
-                ALU.add,
-            )
-            nc.vector.scalar_tensor_tensor(
-                z_planes[:, t, :].rearrange("p (u m) -> p u m", u=PACK),
-                a_ps[t][:].rearrange("p (m u) -> p u m", u=PACK),
-                ga15[:, c],
-                both[:].rearrange("p (u m) -> p u m", u=PACK),
-                ALU.mult,
-                ALU.mult,
-            )
+                tiles.append(bank)
+            return tiles
 
         def mx_tiles(name):
             woven = held.tile([P, N * PACK], BF16, name=name + "_woven", align_bytes=64)
@@ -216,116 +108,216 @@ def tile_picked_hkqedfeshega_none_po_kernel(
             scales = held.tile([P, N], U8, name=name + "_scales", align_bytes=64)
             return woven, codes, scales
 
-        def weave(copy, woven, planes, cols):
+        def weave(copy, woven, tiles, cols):
             copy(
                 woven[:, PACK * cols.start : PACK * cols.stop].rearrange("p (c i t) -> p c t i", i=4, t=PACK),
-                planes[:, :, cols].rearrange("p t (c i) -> p c t i", i=4),
+                tiles[:, :, cols].rearrange("p t (c i) -> p c t i", i=4),
             )
 
         def quantize(woven, codes, scales, cols):
             nc.vector.quantize_mx(
-                out=codes[:, cols].bitcast(FP8X4), scales=scales[:, cols], in_=woven[:, PACK * cols.start : PACK * cols.stop]
+                out=codes[:, cols].bitcast(FP8X4),
+                scales=scales[:, cols],
+                in_=woven[:, PACK * cols.start : PACK * cols.stop],
             )
 
-        whole = slice(0, N)
-        halves = (slice(0, N // 2), slice(N // 2, N))
+        def entries(lst, cols):
+            return lst[:, cols.start // GROUP : cols.stop // GROUP]
 
-        b_stage(2)
-        b_stage(3)
-        for t in range(PACK):
-            a_stats(t)
-        for t in range(PACK):
-            a_finish(t, *a_exps(t))
-        z_woven, z_codes, z_scales = mx_tiles("z")
-        weave(nc.vector.tensor_copy, z_woven, z_planes, whole)
+        xs = cleared_bytes(T, "xs")
+        w2s_raw = cleared_bytes(N, "w2s_raw")
+        w1s_raw = cleared_bytes(N, "w1s_raw")
+        two_l = load_list(two, "two_l")
+        xw = held.tile([P, T], I32, name="xw")
+        xw_src = x_words[0].rearrange("p n r -> p (n r)").bitcast(I32)
+        nc.sync.dma_start(xw[:, 0:X_FIRST], xw_src[:, 0:X_FIRST])
+        xs_rows = x_scales[0].bitcast(I32)
+        rows_by_run = xs_rows.rearrange("(g j) c -> j g c", j=2)
+        rows_by_quad = xs_rows.rearrange("(q j) c -> j q c", j=4)
+        for j in (0, 1):
+            nc.sync.dma_start(xs[j:P:GROUP, :].bitcast(I32), rows_by_run[j])
+        for j in (2, 3):
+            nc.sync.dma_start(xs[j:P:32, :].bitcast(I32), rows_by_quad[j])
+        offs_l = load_list(offs, "offs_l")
+        nc.sync.dma_start(xw[:, X_FIRST:T], xw_src[:, X_FIRST:T])
+        w2_raw = load_weight_words(w2_words, "w2_raw")
+        load_weight_scales(w2s_raw, w2_scales)
+        tau3_t = load_rows(nc.gpsimd, tau3, "tau3_t")
+        n3_l = load_list(n3, "n3_l")
+        w1_raw = load_weight_words(w1_words, "w1_raw")
+        load_weight_scales(w1s_raw, w1_scales)
+        tau_t = load_rows(nc.gpsimd, tau, "tau_t")
+        tau2_t = load_rows(nc.gpsimd, tau2, "tau2_t")
+        n1_l = load_list(n1, "n1_l")
+        n2_l = load_list(n2, "n2_l")
+        n4_l = load_list(n4, "n4_l")
+        n5_l = load_list(n5, "n5_l")
 
-        log_rest = [wins[3][:, 0:N], wins[3][:, N:WIN], ea3[:, 0:N], ea3[:, N : 2 * N]]
-        for t in range(PACK):
-            nc.scalar.activation(log_rest[t], ea3[:, N * t : N * (t + 1)], ACT.Ln, bias=quarter[:], scale=1.0)
-        logit_flat = held.tile([P, PACK * V], F32, name="logit")
-        share_flat = held.tile([P, PACK * V], F32, name="share")
-        logit = logit_flat[:].rearrange("p (t v) -> p t v", t=PACK)
-        share = share_flat[:].rearrange("p (t v) -> p t v", t=PACK)
-        z2_planes = held.tile([P, PACK, V], BF16, name="z2_planes")
+        neg_tau2 = scaled(tau2_t, -1.0, "neg_tau2")
+        quarter = held.tile([P, 1], F32, name="quarter")
+        nc.gpsimd.memset(quarter[:], 0.25)
+
+        windows = [held.tile([P, WINDOW], F32, name="window%d" % t) for t in range(PACK)]
+        for window in windows:
+            nc.vector.memset(window[:, N:WINDOW], 0.0)
+
+        xs_two = held.tile([P, N], U8, name="xs_two", align_bytes=64)
+        nc.vector.tensor_copy(xs_two[:], xs[:].indirect(two_l[:]))
+        xw_two = held.tile([P, N], U32, name="xw_two", align_bytes=64)
+        nc.vector.tensor_copy(xw_two[:], xw[:].bitcast(U32).indirect(two_l[:]))
+        w2_w, w2_s = deal_weight(nc.vector, w2_raw, w2s_raw, "w2")
+
+        xs_offs_raw = held.tile([P, N], U8, name="xs_offs_raw", tag="w2s_raw", align_bytes=64)
+        nc.vector.tensor_copy(xs_offs_raw[:], xs[:].indirect(offs_l[:]))
+        xs_offs = held.tile([P, N], U8, name="xs_offs", align_bytes=64)
+        nc.vector.tensor_copy(xs_offs[:].bitcast(I32), xs_offs_raw[:].bitcast(I32))
+        for j in (0, 1):
+            nc.sync.dma_start(xs_offs[2 + j : P : 32, :].bitcast(I32), xs_offs_raw[GROUP + j : P : 32, :].bitcast(I32))
+
+        b_ps = product(w2_w, FP4X4, w2_s, xw_two, xs_two, "b", "b_bank")
+
+        top2 = held.tile([P, PACK], F32, name="top2")
+        bias3 = held.tile([P, PACK], F32, name="bias3")
+        ea3 = held.tile([P, PACK, N], F32, name="ea3")
+
+        def fetch_ea3(t):
+            c = slice(t, t + 1)
+            nc.vector.tensor_scalar(windows[t][:, WHOLE], b_ps[t][:], 1.0, None, ALU.mult, ALU.max, accum_out=top2[:, c])
+            nc.vector.tensor_scalar(bias3[:, c], top2[:, c], tau3_t[:, c], -1.0, ALU.mult, ALU.mult)
+            nc.scalar.activation(ea3[:, t, :], windows[t][:].indirect(n3_l[:]), ACT.Exp, bias=bias3[:, c], scale=tau3_t[:, c])
+
+        fetch_ea3(0)
+        fetch_ea3(1)
+
+        w1_w, w1_s = deal_weight(nc.gpsimd, w1_raw, w1s_raw, "w1")
+        xw_offs = held.tile([P, N], U32, name="xw_offs", tag="xw_two", align_bytes=64)
+        nc.vector.tensor_copy(xw_offs[:], xw[:].bitcast(U32).indirect(offs_l[:]))
+        a_ps = product(w1_w, FP4X4, w1_s, xw_offs, xs_offs, "a", "a_bank")
+
+        ga_t = load_rows(nc.sync, ga, "ga_t")
+        gb_t = load_rows(nc.sync, gb, "gb_t")
+        tau4_t = load_rows(nc.sync, tau4, "tau4_t")
+        z_factor = scaled(ga_t, 1.5, "z_factor")
+        z2_factor = scaled(gb_t, 2.0, "z2_factor")
+        neg_tau4 = scaled(tau4_t, -1.0, "neg_tau4")
+
+        fetch_ea3(2)
+        fetch_ea3(3)
+
+        top = held.tile([P, PACK], F32, name="top")
+        low = held.tile([P, PACK], F32, name="low")
+        bias1 = held.tile([P, PACK], F32, name="bias1")
+        bias2 = held.tile([P, PACK], F32, name="bias2")
+        z = held.tile([P, PACK, N], BF16, name="z")
         for t in range(PACK):
             c = slice(t, t + 1)
-            nc.vector.scalar_tensor_tensor(logit[:, t, :], b_ps[t][:], tau3_t[:, c], log_rest[t], ALU.mult, ALU.subtract)
-        quantize(z_woven, z_codes, z_scales, whole)
+            nc.vector.tensor_scalar(windows[t][:, WHOLE], a_ps[t][:], 1.0, None, ALU.mult, ALU.max, accum_out=top[:, c])
+            nc.vector.tensor_reduce(low[:, c], a_ps[t][:], AX.X, ALU.min)
+            nc.vector.tensor_scalar(bias1[:, c], top[:, c], tau_t[:, c], -1.0, ALU.mult, ALU.mult)
+            nc.vector.tensor_scalar(bias2[:, c], low[:, c], tau2_t[:, c], None, ALU.mult)
+        for t in range(PACK):
+            c = slice(t, t + 1)
+            ea = ring.tile([P, N], F32, name="ea")
+            ea2 = ring.tile([P, N], F32, name="ea2")
+            nc.scalar.activation(ea[:], windows[t][:].indirect(n1_l[:]), ACT.Exp, bias=bias1[:, c], scale=tau_t[:, c])
+            nc.scalar.activation(ea2[:], windows[t][:].indirect(n2_l[:]), ACT.Exp, bias=bias2[:, c], scale=neg_tau2[:, c])
+            ea_sum = ring.tile([P, N], F32, name="ea_sum")
+            nc.vector.tensor_tensor(
+                ea_sum[:].rearrange("p (u m) -> p m u", u=PACK),
+                ea[:].rearrange("p (m u) -> p m u", u=PACK),
+                ea2[:].rearrange("p (m u) -> p m u", u=PACK),
+                ALU.add,
+            )
+            nc.vector.scalar_tensor_tensor(
+                z[:, t, :].rearrange("p (u m) -> p u m", u=PACK),
+                a_ps[t][:].rearrange("p (m u) -> p u m", u=PACK),
+                z_factor[:, c],
+                ea_sum[:].rearrange("p (u m) -> p u m", u=PACK),
+                ALU.mult,
+                ALU.mult,
+            )
+        z_woven, z_codes, z_scales = mx_tiles("z")
+        weave(nc.vector.tensor_copy, z_woven, z, WHOLE)
+
+        log_rest = [windows[LAST][:, WHOLE], windows[LAST][:, N:WINDOW], ea3[:, 0, :], ea3[:, 1, :]]
+        for t in range(PACK):
+            nc.scalar.activation(log_rest[t], ea3[:, t, :], ACT.Ln, bias=quarter[:], scale=1.0)
+        logit_pairs = [held.tile([P, WINDOW], F32, name="logit%d" % i) for i in range(2)]
+        logit = [logit_pairs[t // 2][:, N * (t % 2) : N * (t % 2 + 1)] for t in range(PACK)]
+        share = held.tile([P, PACK, N], F32, name="share")
+        z2 = held.tile([P, PACK, N], BF16, name="z2")
+        for t in range(PACK):
+            c = slice(t, t + 1)
+            nc.vector.scalar_tensor_tensor(logit[t], b_ps[t][:], tau3_t[:, c], log_rest[t], ALU.mult, ALU.subtract)
+        quantize(z_woven, z_codes, z_scales, WHOLE)
         z2_woven, z2_codes, z2_scales = mx_tiles("z2")
         for t in range(PACK):
             c = slice(t, t + 1)
-            for cols in halves if t == PACK - 1 else (whole,):
-                nc.scalar.activation(share[:, t, cols], logit[:, t, cols], ACT.Sigmoid, bias=bias3[:, c], scale=1.0)
-                nc.vector.scalar_tensor_tensor(z2_planes[:, t, cols], b_ps[t][:, cols], gb2[:, c], share[:, t, cols], ALU.mult, ALU.mult)
-        weave(nc.scalar.copy, z2_woven, z2_planes, slice(0, SCALAR_WEAVE))
+            for cols in HALVES if t == LAST else (WHOLE,):
+                nc.scalar.activation(share[:, t, cols], logit[t][:, cols], ACT.Sigmoid, bias=bias3[:, c], scale=1.0)
+                nc.vector.scalar_tensor_tensor(
+                    z2[:, t, cols], b_ps[t][:, cols], z2_factor[:, c], share[:, t, cols], ALU.mult, ALU.mult
+                )
+        weave(nc.scalar.copy, z2_woven, z2, slice(0, Z2_SCALAR_COLUMNS))
         warm = held.tile([P, 1], F32, name="warm")
         nc.scalar.activation(warm[:], z2_woven[:, 0:1], ACT.Exp, scale=0.0)
-        weave(nc.vector.tensor_copy, z2_woven, z2_planes, slice(SCALAR_WEAVE, N))
-        quantize(z2_woven, z2_codes, z2_scales, whole)
-        s_ps = []
-        for t in range(PACK):
-            bank = psum.tile([P, V], F32, name="ps%d" % t, tag="pa%d" % t)
-            nc.tensor.matmul_mx(
-                out=bank[:],
-                lhsT=z_codes[:, P * t : P * (t + 1)].bitcast(FP8X4),
-                lhsT_scale=z_scales[:, P * t : P * (t + 1)],
-                rhs=z2_codes[:].bitcast(FP8X4),
-                rhs_scale=z2_scales[:],
-                start=True,
-                stop=True,
-            )
-            s_ps.append(bank)
+        weave(nc.vector.tensor_copy, z2_woven, z2, slice(Z2_SCALAR_COLUMNS, N // 2))
+        weave(nc.vector.tensor_copy, z2_woven, z2, HALVES[1])
+        for cols in HALVES:
+            quantize(z2_woven, z2_codes, z2_scales, cols)
 
-        res = held.tile([P, PACK, V], F32, name="res")
+        s16_ps = product(z_codes, FP8X4, z_scales, z2_codes, z2_scales, "s16", "a_bank")
+
+        result = held.tile([P, PACK, N], F32, name="result")
         out_rows = out_0.rearrange("(p t) v -> p t v", t=PACK)
-        o_woven, o_codes, o_scales = mx_tiles("o")
-        half_win = [logit_flat, share_flat, wins[1], wins[2]]
-        sq_win = [wins[0], wins[1], wins[0], wins[0]]
-        ea4 = [wins[2][:, 0:N], ea3[:, 0:N], ea3[:, N : 2 * N], ea3[:, 2 * N : 3 * N]]
+        out_woven, out_codes, out_scales = mx_tiles("out")
+        neg_half = [logit_pairs[0], logit_pairs[1], windows[1], windows[2]]
+        sq = [windows[0], windows[1], windows[0], windows[0]]
+        ea4 = [windows[2][:, WHOLE], ea3[:, 0, :], ea3[:, 1, :], ea3[:, 2, :]]
 
         def square(t):
-            nc.scalar.activation(sq_win[t][:, 0:N], s_ps[t][:], ACT.Square, scale=0.0625)
+            nc.scalar.activation(sq[t][:, WHOLE], s16_ps[t][:], ACT.Square, scale=1.0 / 16)
 
         def halve(t):
-            nc.scalar.activation(half_win[t][:, 0:N], s_ps[t][:], ACT.Copy, scale=-0.03125)
+            nc.scalar.activation(neg_half[t][:, WHOLE], s16_ps[t][:], ACT.Copy, scale=-1.0 / 32)
 
-        def decay(t, cols):
-            entries = slice(cols.start // 16, cols.stop // 16)
-            nc.scalar.activation(ea4[t][:, cols], sq_win[t][:].indirect(n4_l[:, entries]), ACT.Exp, scale=neg_tau4[:, t : t + 1])
+        def fetch_ea4(t, cols):
+            nc.scalar.activation(ea4[t][:, cols], sq[t][:].indirect(entries(n4_l, cols)), ACT.Exp, scale=neg_tau4[:, t : t + 1])
 
-        def product(t, cols):
-            prod = ring.tile([P, cols.stop - cols.start], F32, name="both")
-            nc.vector.scalar_tensor_tensor(prod[:], s_ps[t][:, cols], 0.0625, ea4[t][:, cols], ALU.mult, ALU.mult)
-            return prod
-
-        def finish(t, cols=whole):
-            entries = slice(cols.start // 16, cols.stop // 16)
-            prod = product(t, cols)
-            nc.vector.tensor_tensor(res[:, t, cols], half_win[t][:].indirect(n5_l[:, entries]), prod[:], ALU.add)
-            nc.sync.dma_start(out_rows[:, t, cols], res[:, t, cols])
+        def finish(t):
+            s_ea4 = ring.tile([P, N], F32, name="s_ea4", tag="ea_sum")
+            for cols in HALVES:
+                nc.vector.scalar_tensor_tensor(s_ea4[:, cols], s16_ps[t][:, cols], 1.0 / 16, ea4[t][:, cols], ALU.mult, ALU.mult)
+            for cols in HALVES:
+                nc.vector.tensor_tensor(result[:, t, cols], neg_half[t][:].indirect(entries(n5_l, cols)), s_ea4[:, cols], ALU.add)
+            for cols in HALVES if t == LAST else (WHOLE,):
+                nc.sync.dma_start(out_rows[:, t, cols], result[:, t, cols])
 
         square(0)
-        for t in range(2):
-            nc.vector.tensor_scalar(half_win[t][:, 0:N], s_ps[t][:], -0.03125, None, ALU.mult)
-        nc.vector.scalar_tensor_tensor(sq_win[1][:, 0:N], s_ps[1][:], -0.125, half_win[1][:, 0:N], ALU.mult, ALU.mult)
-        decay(0, whole)
-        decay(1, whole)
+        for t in (0, 1):
+            nc.vector.tensor_scalar(neg_half[t][:, WHOLE], s16_ps[t][:], -1.0 / 32, None, ALU.mult)
+        nc.vector.scalar_tensor_tensor(sq[1][:, WHOLE], s16_ps[1][:], -1.0 / 8, neg_half[1][:, WHOLE], ALU.mult, ALU.mult)
+        fetch_ea4(0, WHOLE)
+        fetch_ea4(1, WHOLE)
         finish(0)
         square(2)
         halve(2)
-        decay(2, whole)
+        fetch_ea4(2, WHOLE)
         finish(1)
         square(3)
         halve(3)
-        for cols in halves:
-            decay(3, cols)
+        for cols in HALVES:
+            fetch_ea4(3, cols)
         finish(2)
-        for cols in halves:
-            finish(3, cols)
-        weave(nc.scalar.copy, o_woven, res, halves[0])
-        weave(nc.vector.tensor_copy, o_woven, res, halves[1])
-        quantize(o_woven, o_codes, o_scales, whole)
-        nc.sync.dma_start(out_1[0].rearrange("p c r -> p (c r)").bitcast(I32), o_codes[:].bitcast(I32))
-        sc_rows = out_2[0].bitcast(I32)
-        for q in range(4):
-            (nc.scalar, nc.sync)[q % 2].dma_start(sc_rows[4 * q : 4 * q + 4, :], o_scales[32 * q : 32 * q + 4, :].bitcast(I32))
+        finish(3)
+
+        weave(nc.scalar.copy, out_woven, result, HALVES[0])
+        weave(nc.vector.tensor_copy, out_woven, result, HALVES[1])
+        out_words = out_1[0].rearrange("p c r -> p (c r)").bitcast(I32)
+        for cols in HALVES:
+            quantize(out_woven, out_codes, out_scales, cols)
+            nc.sync.dma_start(out_words[:, cols], out_codes[:, cols].bitcast(I32))
+        out_scale_rows = out_2[0].bitcast(I32)
+        for q in range(QUADS):
+            queue = nc.scalar if q % 2 == 0 else nc.sync
+            queue.dma_start(out_scale_rows[4 * q : 4 * q + 4, :], out_scales[32 * q : 32 * q + 4, :].bitcast(I32))

from contextlib import ExitStack

import concourse.mybir as mybir

T = 2048
N = 512
FLOPS = 3 * 2 * N * N * N

F32 = mybir.dt.float32
BF16 = mybir.dt.bfloat16
I32 = mybir.dt.int32
U32 = mybir.dt.uint32
U16 = mybir.dt.uint16
U8 = mybir.dt.uint8
FP8X4 = mybir.dt.float8_e4m3fn_x4
FP4X4 = mybir.dt.float4_e2m1fn_x4
ALU = mybir.AluOpType
ACT = mybir.ActivationFunctionType
AX = mybir.AxisListType

P = 128
PACK = 4
QUADS = 4
GROUP = 16
LAST = PACK - 1
WINDOW = 2 * N
X_FIRST = 512
Z2_SCALAR_COLUMNS = 192

WHOLE = slice(0, N)
HALVES = (slice(0, N // 2), slice(N // 2, N))


def tile_picked_hkqedfeshega_none_po_kernel(
    tc, x_words, x_scales, w1_words, w1_scales, w2_words, w2_scales,
    tau, tau2, tau3, ga, gb, tau4, offs, two, n1, n2, n3, n4, n5,
    out_0, out_1, out_2,
):
    nc = tc.nc
    with ExitStack() as ctx:
        held = ctx.enter_context(tc.tile_pool(name="held", bufs=1))
        ring = ctx.enter_context(tc.tile_pool(name="ring", bufs=PACK))
        psum = ctx.enter_context(tc.psum_pool(name="psum", bufs=1))

        def load_list(src, name):
            lst = held.tile([P, N // GROUP], U16, name=name)
            nc.sync.dma_start(lst[:], src)
            return lst

        def load_rows(queue, src, name):
            vec = held.tile([P, PACK], F32, name=name)
            queue.dma_start(vec[:], src.rearrange("(p t) o -> p (t o)", t=PACK))
            return vec

        def scaled(vec, factor, name):
            product = held.tile([P, PACK], F32, name=name)
            nc.gpsimd.tensor_scalar(product[:], vec[:], factor, 0.0, ALU.mult, ALU.add)
            return product

        def cleared_bytes(width, name):
            raw = held.tile([P, width], U8, name=name, align_bytes=64)
            nc.gpsimd.memset(raw[:].bitcast(I32), 0)
            return raw

        def load_weight_words(src, name):
            raw = held.tile([P, 2 * N], U8, name=name)
            nc.sync.dma_start(raw[:].bitcast(I32), src[0].bitcast(I32))
            return raw

        def load_weight_scales(raw, src):
            rows = src[0].bitcast(I32)
            for q in range(QUADS):
                nc.sync.dma_start(raw[32 * q : 32 * q + 4, :].bitcast(I32), rows[4 * q : 4 * q + 4, :])

        def deal_weight(byte_engine, raw_words, raw_scales, name):
            words = held.tile([P, 2 * N], U8, name=name + "_words", align_bytes=64)
            scales = held.tile([P, N], U8, name=name + "_scales", align_bytes=64)
            nc.scalar.copy(
                words[:].bitcast(U16).rearrange("p (t m) -> p m t", t=PACK),
                raw_words[:].bitcast(U16).rearrange("p (m t) -> p m t", t=PACK),
            )
            byte_engine.tensor_copy(
                scales[:].rearrange("p (t m) -> p t m", t=PACK),
                raw_scales[:].rearrange("p (m t) -> p t m", t=PACK),
            )
            return words, scales

        def product(stationary, stationary_dtype, stationary_scales, moving, moving_scales, name, banks):
            width = stationary.shape[1] // PACK
            tiles = []
            for t in range(PACK):
                bank = psum.tile([P, N], F32, name="%s%d" % (name, t), tag="%s%d" % (banks, t))
                nc.tensor.matmul_mx(
                    out=bank[:],
                    lhsT=stationary[:, width * t : width * (t + 1)].bitcast(stationary_dtype),
                    lhsT_scale=stationary_scales[:, P * t : P * (t + 1)],
                    rhs=moving[:].bitcast(FP8X4),
                    rhs_scale=moving_scales[:],
                    start=True,
                    stop=True,
                )
                tiles.append(bank)
            return tiles

        def mx_tiles(name):
            woven = held.tile([P, N * PACK], BF16, name=name + "_woven", align_bytes=64)
            codes = held.tile([P, N], U32, name=name + "_codes", align_bytes=64)
            scales = held.tile([P, N], U8, name=name + "_scales", align_bytes=64)
            return woven, codes, scales

        def weave(copy, woven, tiles, cols):
            copy(
                woven[:, PACK * cols.start : PACK * cols.stop].rearrange("p (c i t) -> p c t i", i=4, t=PACK),
                tiles[:, :, cols].rearrange("p t (c i) -> p c t i", i=4),
            )

        def quantize(woven, codes, scales, cols):
            nc.vector.quantize_mx(
                out=codes[:, cols].bitcast(FP8X4),
                scales=scales[:, cols],
                in_=woven[:, PACK * cols.start : PACK * cols.stop],
            )

        def entries(lst, cols):
            return lst[:, cols.start // GROUP : cols.stop // GROUP]

        xs = cleared_bytes(T, "xs")
        w2s_raw = cleared_bytes(N, "w2s_raw")
        w1s_raw = cleared_bytes(N, "w1s_raw")
        two_l = load_list(two, "two_l")
        xw = held.tile([P, T], I32, name="xw")
        xw_src = x_words[0].rearrange("p n r -> p (n r)").bitcast(I32)
        nc.sync.dma_start(xw[:, 0:X_FIRST], xw_src[:, 0:X_FIRST])
        xs_rows = x_scales[0].bitcast(I32)
        rows_by_run = xs_rows.rearrange("(g j) c -> j g c", j=2)
        rows_by_quad = xs_rows.rearrange("(q j) c -> j q c", j=4)
        for j in (0, 1):
            nc.sync.dma_start(xs[j:P:GROUP, :].bitcast(I32), rows_by_run[j])
        for j in (2, 3):
            nc.sync.dma_start(xs[j:P:32, :].bitcast(I32), rows_by_quad[j])
        offs_l = load_list(offs, "offs_l")
        nc.sync.dma_start(xw[:, X_FIRST:T], xw_src[:, X_FIRST:T])
        w2_raw = load_weight_words(w2_words, "w2_raw")
        load_weight_scales(w2s_raw, w2_scales)
        tau3_t = load_rows(nc.gpsimd, tau3, "tau3_t")
        n3_l = load_list(n3, "n3_l")
        w1_raw = load_weight_words(w1_words, "w1_raw")
        load_weight_scales(w1s_raw, w1_scales)
        tau_t = load_rows(nc.gpsimd, tau, "tau_t")
        tau2_t = load_rows(nc.gpsimd, tau2, "tau2_t")
        n1_l = load_list(n1, "n1_l")
        n2_l = load_list(n2, "n2_l")
        n4_l = load_list(n4, "n4_l")
        n5_l = load_list(n5, "n5_l")

        neg_tau2 = scaled(tau2_t, -1.0, "neg_tau2")
        quarter = held.tile([P, 1], F32, name="quarter")
        nc.gpsimd.memset(quarter[:], 0.25)

        windows = [held.tile([P, WINDOW], F32, name="window%d" % t) for t in range(PACK)]
        for window in windows:
            nc.vector.memset(window[:, N:WINDOW], 0.0)

        xs_two = held.tile([P, N], U8, name="xs_two", align_bytes=64)
        nc.vector.tensor_copy(xs_two[:], xs[:].indirect(two_l[:]))
        xw_two = held.tile([P, N], U32, name="xw_two", align_bytes=64)
        nc.vector.tensor_copy(xw_two[:], xw[:].bitcast(U32).indirect(two_l[:]))
        w2_w, w2_s = deal_weight(nc.vector, w2_raw, w2s_raw, "w2")

        xs_offs_raw = held.tile([P, N], U8, name="xs_offs_raw", tag="w2s_raw", align_bytes=64)
        nc.vector.tensor_copy(xs_offs_raw[:], xs[:].indirect(offs_l[:]))
        xs_offs = held.tile([P, N], U8, name="xs_offs", align_bytes=64)
        nc.vector.tensor_copy(xs_offs[:].bitcast(I32), xs_offs_raw[:].bitcast(I32))
        for j in (0, 1):
            nc.sync.dma_start(xs_offs[2 + j : P : 32, :].bitcast(I32), xs_offs_raw[GROUP + j : P : 32, :].bitcast(I32))

        b_ps = product(w2_w, FP4X4, w2_s, xw_two, xs_two, "b", "b_bank")

        top2 = held.tile([P, PACK], F32, name="top2")
        bias3 = held.tile([P, PACK], F32, name="bias3")
        ea3 = held.tile([P, PACK, N], F32, name="ea3")

        def fetch_ea3(t):
            c = slice(t, t + 1)
            nc.vector.tensor_scalar(windows[t][:, WHOLE], b_ps[t][:], 1.0, None, ALU.mult, ALU.max, accum_out=top2[:, c])
            nc.vector.tensor_scalar(bias3[:, c], top2[:, c], tau3_t[:, c], -1.0, ALU.mult, ALU.mult)
            nc.scalar.activation(ea3[:, t, :], windows[t][:].indirect(n3_l[:]), ACT.Exp, bias=bias3[:, c], scale=tau3_t[:, c])

        fetch_ea3(0)
        fetch_ea3(1)

        w1_w, w1_s = deal_weight(nc.gpsimd, w1_raw, w1s_raw, "w1")
        xw_offs = held.tile([P, N], U32, name="xw_offs", tag="xw_two", align_bytes=64)
        nc.vector.tensor_copy(xw_offs[:], xw[:].bitcast(U32).indirect(offs_l[:]))
        a_ps = product(w1_w, FP4X4, w1_s, xw_offs, xs_offs, "a", "a_bank")

        ga_t = load_rows(nc.sync, ga, "ga_t")
        gb_t = load_rows(nc.sync, gb, "gb_t")
        tau4_t = load_rows(nc.sync, tau4, "tau4_t")
        z_factor = scaled(ga_t, 1.5, "z_factor")
        z2_factor = scaled(gb_t, 2.0, "z2_factor")
        neg_tau4 = scaled(tau4_t, -1.0, "neg_tau4")

        fetch_ea3(2)
        fetch_ea3(3)

        top = held.tile([P, PACK], F32, name="top")
        low = held.tile([P, PACK], F32, name="low")
        bias1 = held.tile([P, PACK], F32, name="bias1")
        bias2 = held.tile([P, PACK], F32, name="bias2")
        z = held.tile([P, PACK, N], BF16, name="z")
        for t in range(PACK):
            c = slice(t, t + 1)
            nc.vector.tensor_scalar(windows[t][:, WHOLE], a_ps[t][:], 1.0, None, ALU.mult, ALU.max, accum_out=top[:, c])
            nc.vector.tensor_reduce(low[:, c], a_ps[t][:], AX.X, ALU.min)
            nc.vector.tensor_scalar(bias1[:, c], top[:, c], tau_t[:, c], -1.0, ALU.mult, ALU.mult)
            nc.vector.tensor_scalar(bias2[:, c], low[:, c], tau2_t[:, c], None, ALU.mult)
        for t in range(PACK):
            c = slice(t, t + 1)
            ea = ring.tile([P, N], F32, name="ea")
            ea2 = ring.tile([P, N], F32, name="ea2")
            nc.scalar.activation(ea[:], windows[t][:].indirect(n1_l[:]), ACT.Exp, bias=bias1[:, c], scale=tau_t[:, c])
            nc.scalar.activation(ea2[:], windows[t][:].indirect(n2_l[:]), ACT.Exp, bias=bias2[:, c], scale=neg_tau2[:, c])
            ea_sum = ring.tile([P, N], F32, name="ea_sum")
            nc.vector.tensor_tensor(
                ea_sum[:].rearrange("p (u m) -> p m u", u=PACK),
                ea[:].rearrange("p (m u) -> p m u", u=PACK),
                ea2[:].rearrange("p (m u) -> p m u", u=PACK),
                ALU.add,
            )
            nc.vector.scalar_tensor_tensor(
                z[:, t, :].rearrange("p (u m) -> p u m", u=PACK),
                a_ps[t][:].rearrange("p (m u) -> p u m", u=PACK),
                z_factor[:, c],
                ea_sum[:].rearrange("p (u m) -> p u m", u=PACK),
                ALU.mult,
                ALU.mult,
            )
        z_woven, z_codes, z_scales = mx_tiles("z")
        weave(nc.vector.tensor_copy, z_woven, z, WHOLE)

        log_rest = [windows[LAST][:, WHOLE], windows[LAST][:, N:WINDOW], ea3[:, 0, :], ea3[:, 1, :]]
        for t in range(PACK):
            nc.scalar.activation(log_rest[t], ea3[:, t, :], ACT.Ln, bias=quarter[:], scale=1.0)
        logit_pairs = [held.tile([P, WINDOW], F32, name="logit%d" % i) for i in range(2)]
        logit = [logit_pairs[t // 2][:, N * (t % 2) : N * (t % 2 + 1)] for t in range(PACK)]
        share = held.tile([P, PACK, N], F32, name="share")
        z2 = held.tile([P, PACK, N], BF16, name="z2")
        for t in range(PACK):
            c = slice(t, t + 1)
            nc.vector.scalar_tensor_tensor(logit[t], b_ps[t][:], tau3_t[:, c], log_rest[t], ALU.mult, ALU.subtract)
        quantize(z_woven, z_codes, z_scales, WHOLE)
        z2_woven, z2_codes, z2_scales = mx_tiles("z2")
        for t in range(PACK):
            c = slice(t, t + 1)
            for cols in HALVES if t == LAST else (WHOLE,):
                nc.scalar.activation(share[:, t, cols], logit[t][:, cols], ACT.Sigmoid, bias=bias3[:, c], scale=1.0)
                nc.vector.scalar_tensor_tensor(
                    z2[:, t, cols], b_ps[t][:, cols], z2_factor[:, c], share[:, t, cols], ALU.mult, ALU.mult
                )
        weave(nc.scalar.copy, z2_woven, z2, slice(0, Z2_SCALAR_COLUMNS))
        warm = held.tile([P, 1], F32, name="warm")
        nc.scalar.activation(warm[:], z2_woven[:, 0:1], ACT.Exp, scale=0.0)
        weave(nc.vector.tensor_copy, z2_woven, z2, slice(Z2_SCALAR_COLUMNS, N // 2))
        weave(nc.vector.tensor_copy, z2_woven, z2, HALVES[1])
        for cols in HALVES:
            quantize(z2_woven, z2_codes, z2_scales, cols)

        s16_ps = product(z_codes, FP8X4, z_scales, z2_codes, z2_scales, "s16", "a_bank")

        result = held.tile([P, PACK, N], F32, name="result")
        out_rows = out_0.rearrange("(p t) v -> p t v", t=PACK)
        out_woven, out_codes, out_scales = mx_tiles("out")
        neg_half = [logit_pairs[0], logit_pairs[1], windows[1], windows[2]]
        sq = [windows[0], windows[1], windows[0], windows[0]]
        ea4 = [windows[2][:, WHOLE], ea3[:, 0, :], ea3[:, 1, :], ea3[:, 2, :]]

        def square(t):
            nc.scalar.activation(sq[t][:, WHOLE], s16_ps[t][:], ACT.Square, scale=1.0 / 16)

        def halve(t):
            nc.scalar.activation(neg_half[t][:, WHOLE], s16_ps[t][:], ACT.Copy, scale=-1.0 / 32)

        def fetch_ea4(t, cols):
            nc.scalar.activation(ea4[t][:, cols], sq[t][:].indirect(entries(n4_l, cols)), ACT.Exp, scale=neg_tau4[:, t : t + 1])

        def finish(t):
            s_ea4 = ring.tile([P, N], F32, name="s_ea4", tag="ea_sum")
            for cols in HALVES:
                nc.vector.scalar_tensor_tensor(s_ea4[:, cols], s16_ps[t][:, cols], 1.0 / 16, ea4[t][:, cols], ALU.mult, ALU.mult)
            for cols in HALVES:
                nc.vector.tensor_tensor(result[:, t, cols], neg_half[t][:].indirect(entries(n5_l, cols)), s_ea4[:, cols], ALU.add)
            for cols in HALVES if t == LAST else (WHOLE,):
                nc.sync.dma_start(out_rows[:, t, cols], result[:, t, cols])

        square(0)
        for t in (0, 1):
            nc.vector.tensor_scalar(neg_half[t][:, WHOLE], s16_ps[t][:], -1.0 / 32, None, ALU.mult)
        nc.vector.scalar_tensor_tensor(sq[1][:, WHOLE], s16_ps[1][:], -1.0 / 8, neg_half[1][:, WHOLE], ALU.mult, ALU.mult)
        fetch_ea4(0, WHOLE)
        fetch_ea4(1, WHOLE)
        finish(0)
        square(2)
        halve(2)
        fetch_ea4(2, WHOLE)
        finish(1)
        square(3)
        halve(3)
        for cols in HALVES:
            fetch_ea4(3, cols)
        finish(2)
        finish(3)

        weave(nc.scalar.copy, out_woven, result, HALVES[0])
        weave(nc.vector.tensor_copy, out_woven, result, HALVES[1])
        out_words = out_1[0].rearrange("p c r -> p (c r)").bitcast(I32)
        for cols in HALVES:
            quantize(out_woven, out_codes, out_scales, cols)
            nc.sync.dma_start(out_words[:, cols], out_codes[:, cols].bitcast(I32))
        out_scale_rows = out_2[0].bitcast(I32)
        for q in range(QUADS):
            queue = nc.scalar if q % 2 == 0 else nc.sync
            queue.dma_start(out_scale_rows[4 * q : 4 * q + 4, :], out_scales[32 * q : 32 * q + 4, :].bitcast(I32))
